import numpy as np
import ml_dtypes

BF16 = ml_dtypes.bfloat16


def bf(x):
    return np.asarray(x, np.float32).astype(BF16)


def f32(x):
    return np.asarray(x, np.float32)


def f64(x):
    return np.asarray(x).astype(np.float64)


def striped(idx):
    return np.tile(idx.reshape(-1, 16).T, (8, 1))


def rows(idx, k):
    return np.tile(idx, (k, 1))


def look(tab, idx):
    return np.take_along_axis(f64(tab), rows(idx, len(tab)), axis=1)


K, S, V, N = 128, 256, 64, 64


def setup_inputs():
    return {"tab": f32(np.random.standard_normal((K, S))), "y": f32(np.random.standard_normal((K, V))), "offs": striped(np.random.permutation(S)[:N])}


def reference(tab, y, offs):
    idx = offs[:16].T.reshape(-1)
    t = look(tab, idx)
    x = np.maximum(t, 0.0) * f64(y)
    return x

@@ -1,0 +1,29 @@
+import concourse.mybir as mybir
+
+ROWS, TABLE_COLUMNS, PICKED = 128, 256, 64
+F32, U16 = mybir.dt.float32, mybir.dt.uint16
+
+FLOPS = 2 * ROWS * PICKED
+
+
+def tile_lookup_gate_relu_out_kernel(tc, tab, y, offs, out):
+    nc = tc.nc
+    with tc.tile_pool(name="held", bufs=1) as held:
+        offsets = held.tile([ROWS, PICKED // 16], U16)
+        table = held.tile([ROWS, TABLE_COLUMNS], F32)
+        stream = held.tile([ROWS, PICKED], F32)
+        gate = held.tile([ROWS, PICKED], F32)
+        product = held.tile([ROWS, PICKED], F32)
+
+        nc.sync.dma_start(table[:], tab)
+        nc.sync.dma_start(offsets[:], offs)
+        nc.sync.dma_start(stream[:], y)
+
+        zero = held.tile([ROWS, 1], F32)
+        warmed = held.tile([ROWS, 1], F32)
+        nc.vector.memset(zero[:], 0.0)
+        nc.scalar.activation(warmed[:], zero[:], mybir.ActivationFunctionType.Relu)
+
+        nc.scalar.activation(gate[:], table[:].indirect(offsets[:]), mybir.ActivationFunctionType.Relu)
+        nc.vector.tensor_tensor(product[:], gate[:], stream[:], mybir.AluOpType.mult)
+        nc.sync.dma_start(out, product[:])

@@ -1,7 +1,8 @@
 import concourse.mybir as mybir
 
 ROWS, TABLE_COLUMNS, PICKED = 128, 256, 64
-F32, U16 = mybir.dt.float32, mybir.dt.uint16
+F32, U16, U32 = mybir.dt.float32, mybir.dt.uint16, mybir.dt.uint32
+RELU, COPY = mybir.ActivationFunctionType.Relu, mybir.ActivationFunctionType.Copy
 
 FLOPS = 2 * ROWS * PICKED
 
@@ -19,11 +20,9 @@ def tile_lookup_gate_relu_out_kernel(tc, tab, y, offs, out):
         nc.sync.dma_start(offsets[:], offs)
         nc.sync.dma_start(stream[:], y)
 
-        zero = held.tile([ROWS, 1], F32)
-        warmed = held.tile([ROWS, 1], F32)
-        nc.vector.memset(zero[:], 0.0)
-        nc.scalar.activation(warmed[:], zero[:], mybir.ActivationFunctionType.Relu)
+        warmed = held.tile([ROWS, 1], U32)
+        nc.scalar.activation(warmed[:], warmed[:], COPY, scale=0.0)
 
-        nc.scalar.activation(gate[:], table[:].indirect(offsets[:]), mybir.ActivationFunctionType.Relu)
-        nc.vector.tensor_tensor(product[:], gate[:], stream[:], mybir.AluOpType.mult)
+        nc.scalar.activation(gate[:], table[:].indirect(offsets[:]), RELU)
+        nc.vector.tensor_tensor(product[:], stream[:], gate[:], mybir.AluOpType.mult)
         nc.sync.dma_start(out, product[:])

@@ -1,6 +1,7 @@
 import concourse.mybir as mybir
 
 ROWS, TABLE_COLUMNS, PICKED = 128, 256, 64
+BURST_BYTES = 256
 F32, U16, U32 = mybir.dt.float32, mybir.dt.uint16, mybir.dt.uint32
 RELU, COPY = mybir.ActivationFunctionType.Relu, mybir.ActivationFunctionType.Copy
 
@@ -11,10 +12,10 @@ def tile_lookup_gate_relu_out_kernel(tc, tab, y, offs, out):
     nc = tc.nc
     with tc.tile_pool(name="held", bufs=1) as held:
         offsets = held.tile([ROWS, PICKED // 16], U16)
-        table = held.tile([ROWS, TABLE_COLUMNS], F32)
-        stream = held.tile([ROWS, PICKED], F32)
+        table = held.tile([ROWS, TABLE_COLUMNS], F32, align_bytes=BURST_BYTES)
+        stream = held.tile([ROWS, PICKED], F32, align_bytes=BURST_BYTES)
+        product = held.tile([ROWS, PICKED], F32, align_bytes=BURST_BYTES)
         gate = held.tile([ROWS, PICKED], F32)
-        product = held.tile([ROWS, PICKED], F32)
 
         nc.sync.dma_start(table[:], tab)
         nc.sync.dma_start(offsets[:], offs)
@@ -24,5 +25,5 @@ def tile_lookup_gate_relu_out_kernel(tc, tab, y, offs, out):
         nc.scalar.activation(warmed[:], warmed[:], COPY, scale=0.0)
 
         nc.scalar.activation(gate[:], table[:].indirect(offsets[:]), RELU)
-        nc.vector.tensor_tensor(product[:], stream[:], gate[:], mybir.AluOpType.mult)
+        nc.vector.tensor_tensor(product[:], gate[:], stream[:], mybir.AluOpType.mult)
         nc.sync.dma_start(out, product[:])

@@ -2,7 +2,7 @@ import concourse.mybir as mybir
 
 ROWS, TABLE_COLUMNS, PICKED = 128, 256, 64
 BURST_BYTES = 256
-F32, U16, U32 = mybir.dt.float32, mybir.dt.uint16, mybir.dt.uint32
+F32, U16 = mybir.dt.float32, mybir.dt.uint16
 RELU, COPY = mybir.ActivationFunctionType.Relu, mybir.ActivationFunctionType.Copy
 
 FLOPS = 2 * ROWS * PICKED
@@ -21,9 +21,13 @@ def tile_lookup_gate_relu_out_kernel(tc, tab, y, offs, out):
         nc.sync.dma_start(offsets[:], offs)
         nc.sync.dma_start(stream[:], y)
 
-        warmed = held.tile([ROWS, 1], U32)
-        nc.scalar.activation(warmed[:], warmed[:], COPY, scale=0.0)
+        seed = held.tile([ROWS, 1], F32)
+        zero = held.tile([ROWS, 1], F32)
+        nc.vector.memset(seed[:], 0.0)
+        nc.scalar.activation(zero[:], seed[:], COPY)
 
         nc.scalar.activation(gate[:], table[:].indirect(offsets[:]), RELU)
-        nc.vector.tensor_tensor(product[:], gate[:], stream[:], mybir.AluOpType.mult)
+        nc.vector.scalar_tensor_tensor(
+            product[:], gate[:], zero[:], stream[:], mybir.AluOpType.add, mybir.AluOpType.mult
+        )
         nc.sync.dma_start(out, product[:])

@@ -2,7 +2,7 @@ import concourse.mybir as mybir
 
 ROWS, TABLE_COLUMNS, PICKED = 128, 256, 64
 BURST_BYTES = 256
-F32, U16 = mybir.dt.float32, mybir.dt.uint16
+F32, U16, U32 = mybir.dt.float32, mybir.dt.uint16, mybir.dt.uint32
 RELU, COPY = mybir.ActivationFunctionType.Relu, mybir.ActivationFunctionType.Copy
 
 FLOPS = 2 * ROWS * PICKED
@@ -21,10 +21,8 @@ def tile_lookup_gate_relu_out_kernel(tc, tab, y, offs, out):
         nc.sync.dma_start(offsets[:], offs)
         nc.sync.dma_start(stream[:], y)
 
-        seed = held.tile([ROWS, 1], F32)
         zero = held.tile([ROWS, 1], F32)
-        nc.vector.memset(seed[:], 0.0)
-        nc.scalar.activation(zero[:], seed[:], COPY)
+        nc.scalar.activation(zero[:], table[:, 0:1].bitcast(U32), COPY, scale=0.0)
 
         nc.scalar.activation(gate[:], table[:].indirect(offsets[:]), RELU)
         nc.vector.scalar_tensor_tensor(

@@ -2,10 +2,15 @@ import concourse.mybir as mybir
 
 ROWS, TABLE_COLUMNS, PICKED = 128, 256, 64
 BURST_BYTES = 256
+RUN = 4
 F32, U16, U32 = mybir.dt.float32, mybir.dt.uint16, mybir.dt.uint32
 RELU, COPY = mybir.ActivationFunctionType.Relu, mybir.ActivationFunctionType.Copy
 
 FLOPS = 2 * ROWS * PICKED
+
+
+def dealt(rows):
+    return rows.rearrange("(d c) f -> c d f", d=RUN)
 
 
 def tile_lookup_gate_relu_out_kernel(tc, tab, y, offs, out):
@@ -17,9 +22,9 @@ def tile_lookup_gate_relu_out_kernel(tc, tab, y, offs, out):
         product = held.tile([ROWS, PICKED], F32, align_bytes=BURST_BYTES)
         gate = held.tile([ROWS, PICKED], F32)
 
-        nc.sync.dma_start(table[:], tab)
+        nc.sync.dma_start(table[:], dealt(tab))
         nc.sync.dma_start(offsets[:], offs)
-        nc.sync.dma_start(stream[:], y)
+        nc.sync.dma_start(stream[:], dealt(y))
 
         zero = held.tile([ROWS, 1], F32)
         nc.scalar.activation(zero[:], table[:, 0:1].bitcast(U32), COPY, scale=0.0)
@@ -28,4 +33,4 @@ def tile_lookup_gate_relu_out_kernel(tc, tab, y, offs, out):
         nc.vector.scalar_tensor_tensor(
             product[:], gate[:], zero[:], stream[:], mybir.AluOpType.add, mybir.AluOpType.mult
         )
-        nc.sync.dma_start(out, product[:])
+        nc.sync.dma_start(dealt(out), product[:])

@@ -3,7 +3,7 @@ import concourse.mybir as mybir
 ROWS, TABLE_COLUMNS, PICKED = 128, 256, 64
 BURST_BYTES = 256
 RUN = 4
-F32, U16, U32 = mybir.dt.float32, mybir.dt.uint16, mybir.dt.uint32
+F32, U16 = mybir.dt.float32, mybir.dt.uint16
 RELU, COPY = mybir.ActivationFunctionType.Relu, mybir.ActivationFunctionType.Copy
 
 FLOPS = 2 * ROWS * PICKED
@@ -26,8 +26,13 @@ def tile_lookup_gate_relu_out_kernel(tc, tab, y, offs, out):
         nc.sync.dma_start(offsets[:], offs)
         nc.sync.dma_start(stream[:], dealt(y))
 
+        seed = held.tile([ROWS, 1], F32)
         zero = held.tile([ROWS, 1], F32)
-        nc.scalar.activation(zero[:], table[:, 0:1].bitcast(U32), COPY, scale=0.0)
+        nc.vector.memset(seed[:], 0.0)
+        nc.scalar.activation(zero[:], seed[:], COPY)
+
+        unread = held.tile([ROWS, 1], F32)
+        nc.scalar.copy(unread[:], table[:, 0:1])
 
         nc.scalar.activation(gate[:], table[:].indirect(offsets[:]), RELU)
         nc.vector.scalar_tensor_tensor(

@@ -4,7 +4,7 @@ ROWS, TABLE_COLUMNS, PICKED = 128, 256, 64
 BURST_BYTES = 256
 RUN = 4
 F32, U16 = mybir.dt.float32, mybir.dt.uint16
-RELU, COPY = mybir.ActivationFunctionType.Relu, mybir.ActivationFunctionType.Copy
+RELU = mybir.ActivationFunctionType.Relu
 
 FLOPS = 2 * ROWS * PICKED
 
@@ -26,16 +26,9 @@ def tile_lookup_gate_relu_out_kernel(tc, tab, y, offs, out):
         nc.sync.dma_start(offsets[:], offs)
         nc.sync.dma_start(stream[:], dealt(y))
 
-        seed = held.tile([ROWS, 1], F32)
-        zero = held.tile([ROWS, 1], F32)
-        nc.vector.memset(seed[:], 0.0)
-        nc.scalar.activation(zero[:], seed[:], COPY)
-
-        unread = held.tile([ROWS, 1], F32)
-        nc.scalar.copy(unread[:], table[:, 0:1])
+        unread = held.tile([32, 1], F32)
+        nc.scalar.copy(unread[:], table[0:32, 0:1])
 
         nc.scalar.activation(gate[:], table[:].indirect(offsets[:]), RELU)
-        nc.vector.scalar_tensor_tensor(
-            product[:], gate[:], zero[:], stream[:], mybir.AluOpType.add, mybir.AluOpType.mult
-        )
+        nc.vector.tensor_tensor(product[:], gate[:], stream[:], mybir.AluOpType.mult)
         nc.sync.dma_start(dealt(out), product[:])

import concourse.mybir as mybir

ROWS, TABLE_COLUMNS, PICKED = 128, 256, 64
BURST_BYTES = 256
RUN = 4
F32, U16 = mybir.dt.float32, mybir.dt.uint16
RELU = mybir.ActivationFunctionType.Relu

FLOPS = 2 * ROWS * PICKED


def dealt(rows):
    return rows.rearrange("(d c) f -> c d f", d=RUN)


def tile_lookup_gate_relu_out_kernel(tc, tab, y, offs, out):
    nc = tc.nc
    with tc.tile_pool(name="held", bufs=1) as held:
        offsets = held.tile([ROWS, PICKED // 16], U16)
        table = held.tile([ROWS, TABLE_COLUMNS], F32, align_bytes=BURST_BYTES)
        stream = held.tile([ROWS, PICKED], F32, align_bytes=BURST_BYTES)
        product = held.tile([ROWS, PICKED], F32, align_bytes=BURST_BYTES)
        gate = held.tile([ROWS, PICKED], F32)

        nc.sync.dma_start(table[:], dealt(tab))
        nc.sync.dma_start(offsets[:], offs)
        nc.sync.dma_start(stream[:], dealt(y))

        unread = held.tile([32, 1], F32)
        nc.scalar.copy(unread[:], table[0:32, 0:1])

        nc.scalar.activation(gate[:], table[:].indirect(offsets[:]), RELU)
        nc.vector.tensor_tensor(product[:], gate[:], stream[:], mybir.AluOpType.mult)
        nc.sync.dma_start(dealt(out), product[:])
